import numpy as np
import ml_dtypes


def mxq(x, axis, fmt="e4m3"):
    dtype, down = {"e4m3": (ml_dtypes.float8_e4m3fn, 7), "e5m2": (ml_dtypes.float8_e5m2, 14)}[fmt]
    v = np.moveaxis(np.asarray(x, np.float32).astype(ml_dtypes.bfloat16).astype(np.float64), axis, -1)
    blocks = v.reshape(v.shape[:-1] + (-1, 32))
    amax = np.abs(blocks).max(-1, keepdims=True)
    byte = np.maximum(np.where(amax > 0, np.frexp(amax)[1] - 1 + 127, 0) - down, 1)
    scale = np.exp2(byte - 127.0)
    codes = (blocks / scale).astype(np.float32).astype(dtype).astype(np.float64)
    return np.moveaxis((codes * scale).reshape(v.shape), -1, axis)


WIDE = False


def mx_kscale(k):
    if not WIDE:
        return np.ones(k)
    levels = np.array([10, -10, 5, -5, 0])
    if k % 512:
        return np.exp2(np.random.permutation(np.resize(levels, k // 32))).repeat(32)
    a = np.empty((k // 512, 16))
    for p in range(k // 512):
        a[p, :8] = np.random.permutation(np.resize(levels, 8))
        for g in range(8):
            far = levels[np.abs(levels - a[p, g]) >= 10]
            a[p, g + 8] = far[np.random.randint(len(far))]
    return np.exp2(a.ravel()).repeat(32)


def f64(x):
    return np.asarray(x).astype(np.float64)


def striped(idx):
    return np.tile(idx.reshape(-1, 16).T, (8, 1)).astype(np.uint16)


def unstriped(offs):
    return offs[:16].T.reshape(-1).astype(np.int64)


def striped8(idx):
    return np.concatenate([x.reshape(-1, 16).T for x in idx]).astype(np.uint16)


def runs(offs, k):
    lists = np.stack([offs[16 * r : 16 * r + 16].T.reshape(-1) for r in range(8)]).astype(np.int64)
    return lists[np.arange(k) % 512 // 64]


def pack_weight(w):
    k, n = w.shape
    w = f64(np.asarray(w, np.float32).astype(ml_dtypes.bfloat16)).reshape(k // 32, 32, n)
    amax = np.abs(w).max(1)
    byte = np.clip(np.where(amax > 0, np.frexp(amax)[1] - 1 + 127 - 7, 1), 1, 254)
    scaled = (w * np.exp2(127.0 - byte)[:, None, :]).reshape(k, n).astype(np.float32)
    words = np.ascontiguousarray(scaled.reshape(k // 512, 128, 4, n).transpose(0, 1, 3, 2)).astype(ml_dtypes.float8_e4m3fn).view(np.uint8)
    return words, np.ascontiguousarray(byte.astype(np.uint8).reshape(k // 512, 16, n))


def unpack_weight(words, scales):
    g, p, n, _ = words.shape
    vals = np.ascontiguousarray(words).view(ml_dtypes.float8_e4m3fn).astype(np.float64) * np.repeat(np.exp2(scales.astype(np.float64) - 127.0), 8, axis=1)[..., None]
    return vals.transpose(0, 1, 3, 2).reshape(g * 512, n)


def relu(v):
    return np.maximum(v, 0.0)


K, T, S, V, N, H = 512, 2048, 512, 256, 512, 512


def setup_inputs():
    n = np.random.standard_normal
    s = mx_kscale(K)[:, None]
    u = mx_kscale(H)
    packed_xT = pack_weight(n((K, T)) * s)
    perm = np.stack([np.random.permutation(S) for _ in range(8)])
    return {
        "x_words": packed_xT[0],
        "x_scales": packed_xT[1],
        "w1": (n((K, H)) / np.sqrt(K) / s * u).astype(np.float32),
        "w2": (n((H, H)) / np.sqrt(H) / u[:, None] * u).astype(np.float32),
        "w3": (n((H, N)) / np.sqrt(H) / u[:, None]).astype(np.float32),
        "offs": striped(np.random.permutation(T)[:S]),
        "la": striped8(perm[:, :V]),
        "lb": striped8(perm[:, V:]),
    }


def reference(x_words, x_scales, w1, w2, w3, offs, la, lb):
    xq = unpack_weight(x_words, x_scales)[:, unstriped(offs)]
    y = mxq(f64(w1), 0, "e4m3").T @ xq
    a = y[np.arange(H)[:, None], runs(la, H)]
    b = y[np.arange(H)[:, None], runs(lb, H)]
    z = 0.75 * (a + b)
    h = relu(mxq(f64(w2), 0, "e4m3").T @ mxq(z, 0, "e4m3"))
    df = a - b
    hb = h - df
    ha = h + df
    p = np.zeros((H, S))
    p[np.arange(H)[:, None], runs(la, H)] = ha
    z2 = p.copy()
    z2[np.arange(H)[:, None], runs(lb, H)] = hb
    return mxq(f64(w3), 0, "e4m3").T @ mxq(z2, 0, "e4m3")

@@ -1,0 +1,195 @@
+from contextlib import ExitStack
+
+import concourse.mybir as mybir
+
+K, T, S, V, N, H = 512, 2048, 512, 256, 512, 512
+FLOPS = 2 * K * H * S + 2 * H * H * V + 2 * H * N * S
+
+F32 = mybir.dt.float32
+BF16 = mybir.dt.bfloat16
+I32 = mybir.dt.int32
+U32 = mybir.dt.uint32
+U16 = mybir.dt.uint16
+U8 = mybir.dt.uint8
+FP8X4 = mybir.dt.float8_e4m3fn_x4
+ALU = mybir.AluOpType
+ACT = mybir.ActivationFunctionType
+
+P = 128
+PACK = 4
+HALF = S // 2
+
+
+def tile_picked_unmerge_relu_p_kernel(
+    tc, x_words, x_scales, w1, w2, w3, offs, la, lb, out
+):
+    nc = tc.nc
+    with ExitStack() as ctx:
+        sb = ctx.enter_context(tc.tile_pool(name="sb", bufs=1))
+        psum = ctx.enter_context(tc.psum_pool(name="psum", bufs=1))
+        banks = [psum.tile([P, 512], F32, name=f"bank{b}") for b in range(8)]
+
+        def mx(acc, w_codes, w_scales, m, codes, scales):
+            cols = slice(m * P, (m + 1) * P)
+            nc.tensor.matmul_mx(
+                out=acc,
+                lhsT=w_codes[:, cols].bitcast(FP8X4),
+                lhsT_scale=w_scales[:, cols],
+                rhs=codes.bitcast(FP8X4),
+                rhs_scale=scales,
+                start=True,
+                stop=True,
+            )
+
+        offs_sb = sb.tile([P, S // 16], U16, name="offs_sb")
+        la_sb = sb.tile([P, V // 16], U16, name="la_sb")
+        lb_sb = sb.tile([P, V // 16], U16, name="lb_sb")
+        xs_all = sb.tile([P, T], U8, name="xs_all", align_bytes=64)
+        xw_all = sb.tile([P, T], I32, name="xw_all", align_bytes=64)
+        raw = [sb.tile([P, PACK, 512], F32, name=f"raw{i}") for i in range(3)]
+
+        nc.vector.memset(xs_all[:].bitcast(I32), 0)
+        nc.sync.dma_start(out=raw[0][:], in_=w1.rearrange("(p j) c -> p j c", j=PACK))
+        for q in range(4):
+            nc.sync.dma_start(
+                out=xs_all[32 * q : 32 * q + 4, :].bitcast(I32),
+                in_=x_scales[0, 4 * q : 4 * q + 4, :].bitcast(I32),
+            )
+        nc.sync.dma_start(offs_sb[:], offs)
+        nc.sync.dma_start(out=xw_all[:], in_=x_words[0].rearrange("p c r -> p (c r)").bitcast(I32))
+        nc.sync.dma_start(la_sb[:], la)
+        nc.sync.dma_start(lb_sb[:], lb)
+        nc.sync.dma_start(out=raw[1][:], in_=w2.rearrange("(p j) c -> p j c", j=PACK))
+        nc.sync.dma_start(out=raw[2][:], in_=w3.rearrange("(p j) c -> p j c", j=PACK))
+
+        def dealt(dst, src, m0, m1):
+            return (
+                dst[:].rearrange("p (t m j) -> p m j t", t=PACK, j=PACK)[:, m0:m1],
+                src[:].rearrange("p j (m t) -> p m j t", t=PACK)[:, m0:m1],
+            )
+
+        w1_bf = sb.tile([P, PACK * H], BF16, name="w1_bf", align_bytes=64)
+        w1_codes = sb.tile([P, H], U32, name="w1_codes", align_bytes=64)
+        w1_scales = sb.tile([P, H], U8, name="w1_scales", align_bytes=64)
+        nc.vector.tensor_copy(*dealt(w1_bf, raw[0], 0, 80))
+        nc.scalar.copy(*dealt(w1_bf, raw[0], 80, 128))
+
+        xs = sb.tile([P, S], U8, name="xs", align_bytes=64)
+        nc.vector.tensor_copy(xs[:], xs_all[:].indirect(offs_sb[:]))
+        nc.vector.quantize_mx(out=w1_codes[:].bitcast(FP8X4), scales=w1_scales[:], in_=w1_bf[:])
+
+        xw = [sb.tile([P, HALF], U32, name=f"xw{u}", align_bytes=64) for u in range(2)]
+        y = [sb.tile([P, S], F32, name=f"y{t}") for t in range(PACK)]
+        order = (3, 0, 1, 2)
+        for u in range(2):
+            nc.vector.tensor_copy(xw[u][:], xw_all[:].bitcast(U32).indirect(offs_sb[:, 16 * u : 16 * (u + 1)]))
+        for t0 in (0, 2):
+            for u in range(2):
+                cols = slice(u * HALF, (u + 1) * HALF)
+                for t in (t0, t0 + 1):
+                    bank = banks[PACK * u + t]
+                    mx(bank[:, :HALF], w1_codes, w1_scales, t, xw[u][:], xs[:, cols])
+                    nc.scalar.copy(y[t][:, cols], bank[:, :HALF])
+
+        w2_bf = sb.tile([P, PACK * H], BF16, name="w2_bf", align_bytes=64)
+        w2_codes = sb.tile([P, H], U32, name="w2_codes", align_bytes=64)
+        w2_scales = sb.tile([P, H], U8, name="w2_scales", align_bytes=64)
+        for m0 in range(0, P, 32):
+            nc.scalar.copy(*dealt(w2_bf, raw[1], m0, m0 + 32))
+
+        a = sb.tile([P, PACK, V], F32, name="a")
+        s = sb.tile([P, PACK, V], F32, name="s")
+        for t0 in (0, 2):
+            for t in (t0, t0 + 1):
+                nc.vector.tensor_copy(a[:, t, :], y[t][:].indirect(la_sb[:]))
+            for t in (t0, t0 + 1):
+                nc.vector.tensor_tensor(s[:, t, :], y[t][:].indirect(lb_sb[:]), a[:, t, :], ALU.add)
+        nc.vector.quantize_mx(out=w2_codes[:].bitcast(FP8X4), scales=w2_scales[:], in_=w2_bf[:])
+
+        z_bf = sb.tile([P, V, PACK], BF16, name="z_bf", align_bytes=64)
+        s_by_col = s[:].rearrange("p t v -> p v t")
+        nc.scalar.activation(z_bf[:, :, 0:2], s_by_col[:, :, 0:2], ACT.Copy, scale=0.75)
+        nc.vector.tensor_scalar(z_bf[:, :, 2:4], s_by_col[:, :, 2:4], 0.75, None, ALU.mult)
+        z_codes = sb.tile([P, 1024], U32, name="z_codes", tag="late", align_bytes=64)
+        z_scales = sb.tile([P, V], U8, name="z_scales", align_bytes=64)
+        nc.vector.quantize_mx(
+            out=z_codes[:, :V].bitcast(FP8X4), scales=z_scales[:], in_=z_bf[:].rearrange("p v t -> p (v t)")
+        )
+
+        df = sb.tile([P, PACK, V], F32, name="df")
+        ndf = sb.tile([P, PACK, V], F32, name="ndf")
+        h = sb.tile([P, PACK, V], F32, name="h")
+        for t in order:
+            nc.vector.scalar_tensor_tensor(df[:, t, :], a[:, t, :], 2.0, s[:, t, :], ALU.mult, ALU.subtract)
+        for t in order:
+            mx(banks[t][:, :V], w2_codes, w2_scales, t, z_codes[:, :V], z_scales[:])
+            nc.scalar.activation(h[:, t, :], banks[t][:, :V], ACT.Relu)
+        for t in order:
+            nc.scalar.activation(ndf[:, t, :], df[:, t, :], ACT.Copy, scale=-1.0)
+
+        w3_bf = sb.tile([P, PACK * N], BF16, name="w3_bf", tag="late", align_bytes=64)
+        w3_codes = sb.tile([P, N], U32, name="w3_codes", align_bytes=64)
+        w3_scales = sb.tile([P, N], U8, name="w3_scales", align_bytes=64)
+        for c0 in range(0, P, 64):
+            nc.scalar.copy(
+                w3_bf[:].rearrange("p (c i j) -> p c j i", i=4, j=PACK)[:, c0 : c0 + 64],
+                raw[2][:].rearrange("p j (c i) -> p c j i", i=4)[:, c0 : c0 + 64],
+            )
+
+        z2 = [sb.tile([P, 2 * S if t == 2 else S], F32, name=f"z2_{t}") for t in range(PACK)]
+        z2_bf = sb.tile([P, S, PACK], BF16, name="z2_bf", align_bytes=64)
+
+        def put_a(t):
+            nc.vector.tensor_tensor(z2[t][:].indirect(la_sb[:]), h[:, t, :], df[:, t, :], ALU.add)
+
+        def put_b(t):
+            nc.vector.tensor_tensor(z2[t][:].indirect(lb_sb[:]), h[:, t, :], ndf[:, t, :], ALU.add)
+
+        def weave(t):
+            for u in range(2):
+                cols = slice(u * HALF, (u + 1) * HALF)
+                nc.scalar.copy(z2_bf[:, cols, t], z2[t][:, cols])
+
+        put_a(3)
+        put_a(0)
+        put_b(3)
+        nc.scalar.copy(z2[2][:, S:], z2[3][:])
+        put_a(1)
+        put_b(0)
+        weave(0)
+        nc.vector.quantize_mx(out=w3_codes[:].bitcast(FP8X4), scales=w3_scales[:], in_=w3_bf[:])
+        put_a(2)
+        put_b(1)
+        weave(1)
+        put_b(2)
+
+        pair = z2[2][:].rearrange("p (u c) -> p c u", u=2)
+        pieces = (slice(0, P), slice(P, HALF), slice(HALF, S))
+        for cols in pieces[:2]:
+            nc.vector.tensor_copy(z2_bf[:, cols, 2:4], pair[:, cols, :])
+        nc.scalar.copy(z2_bf[:, HALF:, 2:4], pair[:, HALF:, :])
+
+        z2_codes = sb.tile([P, S], U32, name="z2_codes", align_bytes=64)
+        z2_scales = sb.tile([P, S], U8, name="z2_scales", align_bytes=64)
+        res = [sb.tile([P, PACK, HALF], F32, name=f"res{u}") for u in range(2)]
+        out_v = out.rearrange("(m p) c -> p m c", p=P)
+        for cols in pieces:
+            nc.vector.quantize_mx(
+                out=z2_codes[:, cols].bitcast(FP8X4),
+                scales=z2_scales[:, cols],
+                in_=z2_bf[:, cols, :].rearrange("p c t -> p (c t)"),
+            )
+        for i, cols in enumerate(pieces[:2]):
+            bank = banks[4 + i]
+            for m in range(PACK):
+                mx(bank[:, m * P : (m + 1) * P], w3_codes, w3_scales, m, z2_codes[:, cols], z2_scales[:, cols])
+            copy = nc.scalar.copy if i == 0 else nc.vector.tensor_copy
+            copy(res[0][:, :, cols], bank[:].rearrange("p (m c) -> p m c", m=PACK))
+        nc.sync.dma_start(out=out_v[:, :, :HALF], in_=res[0][:])
+        cols = pieces[2]
+        for m in range(PACK):
+            mx(banks[m][:, :HALF], w3_codes, w3_scales, m, z2_codes[:, cols], z2_scales[:, cols])
+            copy = nc.scalar.copy if m % 2 == 0 else nc.vector.tensor_copy
+            copy(res[1][:, m, :], banks[m][:, :HALF])
+            if m % 2 == 1:
+                nc.sync.dma_start(out=out_v[:, m - 1 : m + 1, cols], in_=res[1][:, m - 1 : m + 1, :])

@@ -18,6 +18,11 @@ ACT = mybir.ActivationFunctionType
 P = 128
 PACK = 4
 HALF = S // 2
+HALVES = (slice(0, HALF), slice(HALF, S))
+M_HALF = P // 2
+W1_VECTOR_SHARE = 40
+W2_PIECES, W3_PIECES = 4, 2
+SCATTER_ORDER = (3, 0, 1, 2)
 
 
 def tile_picked_unmerge_relu_p_kernel(
@@ -26,11 +31,12 @@ def tile_picked_unmerge_relu_p_kernel(
     nc = tc.nc
     with ExitStack() as ctx:
         sb = ctx.enter_context(tc.tile_pool(name="sb", bufs=1))
+        stage = ctx.enter_context(tc.tile_pool(name="stage", bufs=1))
         psum = ctx.enter_context(tc.psum_pool(name="psum", bufs=1))
         banks = [psum.tile([P, 512], F32, name=f"bank{b}") for b in range(8)]
 
-        def mx(acc, w_codes, w_scales, m, codes, scales):
-            cols = slice(m * P, (m + 1) * P)
+        def product(acc, w_codes, w_scales, t, codes, scales):
+            cols = slice(t * P, (t + 1) * P)
             nc.tensor.matmul_mx(
                 out=acc,
                 lhsT=w_codes[:, cols].bitcast(FP8X4),
@@ -41,155 +47,168 @@ def tile_picked_unmerge_relu_p_kernel(
                 stop=True,
             )
 
+        def quantize_weight(codes, scales, rounded, t0, t1):
+            cols = slice(t0 * P, t1 * P)
+            nc.vector.quantize_mx(
+                out=codes[:, cols].bitcast(FP8X4),
+                scales=scales[:, cols],
+                in_=rounded[:, PACK * t0 * P : PACK * t1 * P],
+            )
+
+        def deal_to(rounded):
+            return rounded[:].rearrange("p (t m j) -> p m j t", t=PACK, j=PACK)
+
+        def deal_from(raw):
+            return raw[:].rearrange("p j (m t) -> p m j t", t=PACK)
+
         offs_sb = sb.tile([P, S // 16], U16, name="offs_sb")
         la_sb = sb.tile([P, V // 16], U16, name="la_sb")
         lb_sb = sb.tile([P, V // 16], U16, name="lb_sb")
         xs_all = sb.tile([P, T], U8, name="xs_all", align_bytes=64)
         xw_all = sb.tile([P, T], I32, name="xw_all", align_bytes=64)
-        raw = [sb.tile([P, PACK, 512], F32, name=f"raw{i}") for i in range(3)]
+        w1_raw = [sb.tile([P, PACK, HALF], F32, name=f"w1_raw{u}") for u in range(2)]
+        w2_raw = stage.tile([P, PACK, H], F32, name="w2_raw", offset=0, align_bytes=64)
+        w3_raw = sb.tile([P, PACK, N], F32, name="w3_raw")
 
         nc.vector.memset(xs_all[:].bitcast(I32), 0)
-        nc.sync.dma_start(out=raw[0][:], in_=w1.rearrange("(p j) c -> p j c", j=PACK))
-        for q in range(4):
+        nc.sync.dma_start(offs_sb[:], offs)
+        nc.sync.dma_start(out=xw_all[:], in_=x_words[0].rearrange("p c r -> p (c r)").bitcast(I32))
+        for q in (0, 2, 1, 3):
             nc.sync.dma_start(
                 out=xs_all[32 * q : 32 * q + 4, :].bitcast(I32),
                 in_=x_scales[0, 4 * q : 4 * q + 4, :].bitcast(I32),
             )
-        nc.sync.dma_start(offs_sb[:], offs)
-        nc.sync.dma_start(out=xw_all[:], in_=x_words[0].rearrange("p c r -> p (c r)").bitcast(I32))
+        for u, cols in enumerate(HALVES):
+            nc.sync.dma_start(out=w1_raw[u][:], in_=w1.rearrange("(p j) c -> p j c", j=PACK)[:, :, cols])
         nc.sync.dma_start(la_sb[:], la)
         nc.sync.dma_start(lb_sb[:], lb)
-        nc.sync.dma_start(out=raw[1][:], in_=w2.rearrange("(p j) c -> p j c", j=PACK))
-        nc.sync.dma_start(out=raw[2][:], in_=w3.rearrange("(p j) c -> p j c", j=PACK))
+        nc.sync.dma_start(out=w2_raw[:], in_=w2.rearrange("(p j) c -> p j c", j=PACK))
+        nc.sync.dma_start(out=w3_raw[:], in_=w3.rearrange("(p j) c -> p j c", j=PACK))
 
-        def dealt(dst, src, m0, m1):
-            return (
-                dst[:].rearrange("p (t m j) -> p m j t", t=PACK, j=PACK)[:, m0:m1],
-                src[:].rearrange("p j (m t) -> p m j t", t=PACK)[:, m0:m1],
-            )
+        xw = sb.tile([P, S], U32, name="xw", tag="xw_then_w2", align_bytes=64)
+        xs = sb.tile([P, S], U8, name="xs", align_bytes=64)
+        nc.vector.tensor_copy(xw[:], xw_all[:].bitcast(U32).indirect(offs_sb[:]))
+        nc.vector.tensor_copy(xs[:], xs_all[:].indirect(offs_sb[:]))
 
         w1_bf = sb.tile([P, PACK * H], BF16, name="w1_bf", align_bytes=64)
         w1_codes = sb.tile([P, H], U32, name="w1_codes", align_bytes=64)
         w1_scales = sb.tile([P, H], U8, name="w1_scales", align_bytes=64)
-        nc.vector.tensor_copy(*dealt(w1_bf, raw[0], 0, 80))
-        nc.scalar.copy(*dealt(w1_bf, raw[0], 80, 128))
+        cut = M_HALF + W1_VECTOR_SHARE
+        nc.scalar.copy(deal_to(w1_bf)[:, :M_HALF], deal_from(w1_raw[0]))
+        nc.vector.tensor_copy(deal_to(w1_bf)[:, M_HALF:cut], deal_from(w1_raw[1])[:, :W1_VECTOR_SHARE])
+        nc.scalar.copy(deal_to(w1_bf)[:, cut:], deal_from(w1_raw[1])[:, W1_VECTOR_SHARE:])
+        for t0, t1 in ((0, 1), (1, 2), (2, 4)):
+            quantize_weight(w1_codes, w1_scales, w1_bf, t0, t1)
 
-        xs = sb.tile([P, S], U8, name="xs", align_bytes=64)
-        nc.vector.tensor_copy(xs[:], xs_all[:].indirect(offs_sb[:]))
-        nc.vector.quantize_mx(out=w1_codes[:].bitcast(FP8X4), scales=w1_scales[:], in_=w1_bf[:])
-
-        xw = [sb.tile([P, HALF], U32, name=f"xw{u}", align_bytes=64) for u in range(2)]
         y = [sb.tile([P, S], F32, name=f"y{t}") for t in range(PACK)]
-        order = (3, 0, 1, 2)
-        for u in range(2):
-            nc.vector.tensor_copy(xw[u][:], xw_all[:].bitcast(U32).indirect(offs_sb[:, 16 * u : 16 * (u + 1)]))
-        for t0 in (0, 2):
-            for u in range(2):
-                cols = slice(u * HALF, (u + 1) * HALF)
-                for t in (t0, t0 + 1):
-                    bank = banks[PACK * u + t]
-                    mx(bank[:, :HALF], w1_codes, w1_scales, t, xw[u][:], xs[:, cols])
-                    nc.scalar.copy(y[t][:, cols], bank[:, :HALF])
+        for t in range(PACK):
+            for u, cols in enumerate(HALVES):
+                bank = banks[2 * t + u]
+                product(bank[:, :HALF], w1_codes, w1_scales, t, xw[:, cols], xs[:, cols])
+                copy = nc.vector.tensor_copy if (t, u) == (0, 1) else nc.scalar.copy
+                copy(y[t][:, cols], bank[:, :HALF])
 
-        w2_bf = sb.tile([P, PACK * H], BF16, name="w2_bf", align_bytes=64)
+        w2_bf = sb.tile([P, PACK * H], BF16, name="w2_bf", tag="xw_then_w2", align_bytes=64)
         w2_codes = sb.tile([P, H], U32, name="w2_codes", align_bytes=64)
         w2_scales = sb.tile([P, H], U8, name="w2_scales", align_bytes=64)
-        for m0 in range(0, P, 32):
-            nc.scalar.copy(*dealt(w2_bf, raw[1], m0, m0 + 32))
+        for m0 in range(0, P, P // W2_PIECES):
+            ms = slice(m0, m0 + P // W2_PIECES)
+            nc.scalar.copy(deal_to(w2_bf)[:, ms], deal_from(w2_raw)[:, ms])
 
         a = sb.tile([P, PACK, V], F32, name="a")
-        s = sb.tile([P, PACK, V], F32, name="s")
+        pair_sum = sb.tile([P, PACK, V], F32, name="pair_sum")
         for t0 in (0, 2):
             for t in (t0, t0 + 1):
                 nc.vector.tensor_copy(a[:, t, :], y[t][:].indirect(la_sb[:]))
             for t in (t0, t0 + 1):
-                nc.vector.tensor_tensor(s[:, t, :], y[t][:].indirect(lb_sb[:]), a[:, t, :], ALU.add)
-        nc.vector.quantize_mx(out=w2_codes[:].bitcast(FP8X4), scales=w2_scales[:], in_=w2_bf[:])
+                nc.vector.tensor_tensor(pair_sum[:, t, :], y[t][:].indirect(lb_sb[:]), a[:, t, :], ALU.add)
 
-        z_bf = sb.tile([P, V, PACK], BF16, name="z_bf", align_bytes=64)
-        s_by_col = s[:].rearrange("p t v -> p v t")
-        nc.scalar.activation(z_bf[:, :, 0:2], s_by_col[:, :, 0:2], ACT.Copy, scale=0.75)
-        nc.vector.tensor_scalar(z_bf[:, :, 2:4], s_by_col[:, :, 2:4], 0.75, None, ALU.mult)
-        z_codes = sb.tile([P, 1024], U32, name="z_codes", tag="late", align_bytes=64)
+        quantize_weight(w2_codes, w2_scales, w2_bf, 3, 4)
+        z_bf = stage.tile([P, V, PACK], BF16, name="z_bf", offset=0, align_bytes=64)
+        sum_by_column = pair_sum[:].rearrange("p t v -> p v t")
+        nc.scalar.activation(z_bf[:, :, 0:2], sum_by_column[:, :, 0:2], ACT.Copy, scale=0.75)
+        nc.vector.tensor_scalar(z_bf[:, :, 2:4], sum_by_column[:, :, 2:4], 0.75, None, ALU.mult)
+        quantize_weight(w2_codes, w2_scales, w2_bf, 0, 1)
+        z_codes = sb.tile([P, V], U32, name="z_codes", tag="z_then_w3", align_bytes=64)
         z_scales = sb.tile([P, V], U8, name="z_scales", align_bytes=64)
         nc.vector.quantize_mx(
-            out=z_codes[:, :V].bitcast(FP8X4), scales=z_scales[:], in_=z_bf[:].rearrange("p v t -> p (v t)")
+            out=z_codes[:].bitcast(FP8X4), scales=z_scales[:], in_=z_bf[:].rearrange("p v t -> p (v t)")
         )
+        quantize_weight(w2_codes, w2_scales, w2_bf, 1, 3)
 
-        df = sb.tile([P, PACK, V], F32, name="df")
-        ndf = sb.tile([P, PACK, V], F32, name="ndf")
+        twice_a = stage.tile([P, PACK, V], F32, name="twice_a", offset=PACK * V * 4, align_bytes=64)
+        for t0 in (2, 0):
+            nc.scalar.activation(twice_a[:, t0 : t0 + 2, :], a[:, t0 : t0 + 2, :], ACT.Copy, scale=2.0)
+        df = stage.tile([P, PACK, V], F32, name="df", offset=0, align_bytes=64)
+        neg_df_early = sb.tile([P, 2, V], F32, name="neg_df_early")
+        neg_df = {3: neg_df_early[:, 0, :], 0: neg_df_early[:, 1, :]}
         h = sb.tile([P, PACK, V], F32, name="h")
-        for t in order:
-            nc.vector.scalar_tensor_tensor(df[:, t, :], a[:, t, :], 2.0, s[:, t, :], ALU.mult, ALU.subtract)
-        for t in order:
-            mx(banks[t][:, :V], w2_codes, w2_scales, t, z_codes[:, :V], z_scales[:])
+        for t in SCATTER_ORDER:
+            nc.vector.tensor_tensor(df[:, t, :], twice_a[:, t, :], pair_sum[:, t, :], ALU.subtract)
+        for t in SCATTER_ORDER:
+            product(banks[t][:, :V], w2_codes, w2_scales, t, z_codes[:], z_scales[:])
             nc.scalar.activation(h[:, t, :], banks[t][:, :V], ACT.Relu)
-        for t in order:
-            nc.scalar.activation(ndf[:, t, :], df[:, t, :], ACT.Copy, scale=-1.0)
+        for t in SCATTER_ORDER[:2]:
+            nc.scalar.activation(neg_df[t], df[:, t, :], ACT.Copy, scale=-1.0)
 
-        w3_bf = sb.tile([P, PACK * N], BF16, name="w3_bf", tag="late", align_bytes=64)
-        w3_codes = sb.tile([P, N], U32, name="w3_codes", align_bytes=64)
-        w3_scales = sb.tile([P, N], U8, name="w3_scales", align_bytes=64)
-        for c0 in range(0, P, 64):
-            nc.scalar.copy(
-                w3_bf[:].rearrange("p (c i j) -> p c j i", i=4, j=PACK)[:, c0 : c0 + 64],
-                raw[2][:].rearrange("p j (c i) -> p c j i", i=4)[:, c0 : c0 + 64],
-            )
-
-        z2 = [sb.tile([P, 2 * S if t == 2 else S], F32, name=f"z2_{t}") for t in range(PACK)]
+        z2 = [sb.tile([P, 2 * S if t == 2 else S], F32, name=f"z2_{t}") for t in range(PACK - 1)]
+        z2.append(sb.tile([P, S], F32, name="z2_3", tag="z2_3_then_neg_df_then_w3", align_bytes=64))
         z2_bf = sb.tile([P, S, PACK], BF16, name="z2_bf", align_bytes=64)
 
-        def put_a(t):
+        def scatter_a(t):
             nc.vector.tensor_tensor(z2[t][:].indirect(la_sb[:]), h[:, t, :], df[:, t, :], ALU.add)
 
-        def put_b(t):
-            nc.vector.tensor_tensor(z2[t][:].indirect(lb_sb[:]), h[:, t, :], ndf[:, t, :], ALU.add)
+        def scatter_b(t):
+            nc.vector.tensor_tensor(z2[t][:].indirect(lb_sb[:]), h[:, t, :], neg_df[t], ALU.add)
 
         def weave(t):
-            for u in range(2):
-                cols = slice(u * HALF, (u + 1) * HALF)
+            for cols in HALVES:
                 nc.scalar.copy(z2_bf[:, cols, t], z2[t][:, cols])
 
-        put_a(3)
-        put_a(0)
-        put_b(3)
+        scatter_a(3)
+        scatter_a(0)
+        scatter_b(3)
         nc.scalar.copy(z2[2][:, S:], z2[3][:])
-        put_a(1)
-        put_b(0)
+        neg_df_late = sb.tile([P, 2, V], F32, name="neg_df_late", tag="z2_3_then_neg_df_then_w3", align_bytes=64)
+        nc.scalar.activation(neg_df_late[:], df[:, 1:3, :], ACT.Copy, scale=-1.0)
+        neg_df[1], neg_df[2] = neg_df_late[:, 0, :], neg_df_late[:, 1, :]
+        w3_bf = sb.tile([P, PACK * N], BF16, name="w3_bf", tag="z_then_w3", align_bytes=64)
+        for c0 in range(0, P, P // W3_PIECES):
+            cs = slice(c0, c0 + P // W3_PIECES)
+            nc.scalar.copy(
+                w3_bf[:].rearrange("p (c i j) -> p c j i", i=4, j=PACK)[:, cs],
+                w3_raw[:].rearrange("p j (c i) -> p c j i", i=4)[:, cs],
+            )
+        scatter_a(1)
+        scatter_b(0)
         weave(0)
-        nc.vector.quantize_mx(out=w3_codes[:].bitcast(FP8X4), scales=w3_scales[:], in_=w3_bf[:])
-        put_a(2)
-        put_b(1)
+        scatter_a(2)
+        scatter_b(1)
         weave(1)
-        put_b(2)
+        scatter_b(2)
 
-        pair = z2[2][:].rearrange("p (u c) -> p c u", u=2)
-        pieces = (slice(0, P), slice(P, HALF), slice(HALF, S))
-        for cols in pieces[:2]:
-            nc.vector.tensor_copy(z2_bf[:, cols, 2:4], pair[:, cols, :])
-        nc.scalar.copy(z2_bf[:, HALF:, 2:4], pair[:, HALF:, :])
+        w3_codes = sb.tile([P, N], U32, name="w3_codes", tag="z2_3_then_neg_df_then_w3", align_bytes=64)
+        w3_scales = sb.tile([P, N], U8, name="w3_scales", align_bytes=64)
+        quantize_weight(w3_codes, w3_scales, w3_bf, 0, 1)
+        tiles_2_3 = z2[2][:].rearrange("p (u c) -> p c u", u=2)
+        nc.vector.tensor_copy(z2_bf[:, :HALF, 2:4], tiles_2_3[:, :HALF, :])
+        nc.scalar.copy(z2_bf[:, HALF:, 2:4], tiles_2_3[:, HALF:, :])
 
         z2_codes = sb.tile([P, S], U32, name="z2_codes", align_bytes=64)
         z2_scales = sb.tile([P, S], U8, name="z2_scales", align_bytes=64)
-        res = [sb.tile([P, PACK, HALF], F32, name=f"res{u}") for u in range(2)]
-        out_v = out.rearrange("(m p) c -> p m c", p=P)
-        for cols in pieces:
+        for cols, (t0, t1) in zip(HALVES, ((1, 2), (2, 4))):
+            quantize_weight(w3_codes, w3_scales, w3_bf, t0, t1)
             nc.vector.quantize_mx(
                 out=z2_codes[:, cols].bitcast(FP8X4),
                 scales=z2_scales[:, cols],
                 in_=z2_bf[:, cols, :].rearrange("p c t -> p (c t)"),
             )
-        for i, cols in enumerate(pieces[:2]):
-            bank = banks[4 + i]
-            for m in range(PACK):
-                mx(bank[:, m * P : (m + 1) * P], w3_codes, w3_scales, m, z2_codes[:, cols], z2_scales[:, cols])
-            copy = nc.scalar.copy if i == 0 else nc.vector.tensor_copy
-            copy(res[0][:, :, cols], bank[:].rearrange("p (m c) -> p m c", m=PACK))
-        nc.sync.dma_start(out=out_v[:, :, :HALF], in_=res[0][:])
-        cols = pieces[2]
-        for m in range(PACK):
-            mx(banks[m][:, :HALF], w3_codes, w3_scales, m, z2_codes[:, cols], z2_scales[:, cols])
-            copy = nc.scalar.copy if m % 2 == 0 else nc.vector.tensor_copy
-            copy(res[1][:, m, :], banks[m][:, :HALF])
-            if m % 2 == 1:
-                nc.sync.dma_start(out=out_v[:, m - 1 : m + 1, cols], in_=res[1][:, m - 1 : m + 1, :])
+
+        for u, cols in enumerate(HALVES):
+            for t in range(PACK):
+                result = sb.tile([P, HALF], F32, name=f"result{u}{t}")
+                bank = banks[PACK * u + t]
+                product(bank[:, :HALF], w3_codes, w3_scales, t, z2_codes[:, cols], z2_scales[:, cols])
+                copy = nc.scalar.copy if t % 2 == 0 else nc.vector.tensor_copy
+                copy(result[:], bank[:, :HALF])
+                nc.sync.dma_start(out=out[t * P : (t + 1) * P, cols], in_=result[:])

from contextlib import ExitStack

import concourse.mybir as mybir

K, T, S, V, N, H = 512, 2048, 512, 256, 512, 512
FLOPS = 2 * K * H * S + 2 * H * H * V + 2 * H * N * S

F32 = mybir.dt.float32
BF16 = mybir.dt.bfloat16
I32 = mybir.dt.int32
U32 = mybir.dt.uint32
U16 = mybir.dt.uint16
U8 = mybir.dt.uint8
FP8X4 = mybir.dt.float8_e4m3fn_x4
ALU = mybir.AluOpType
ACT = mybir.ActivationFunctionType

P = 128
PACK = 4
HALF = S // 2
HALVES = (slice(0, HALF), slice(HALF, S))
M_HALF = P // 2
W1_VECTOR_SHARE = 40
W2_PIECES, W3_PIECES = 4, 2
SCATTER_ORDER = (3, 0, 1, 2)


def tile_picked_unmerge_relu_p_kernel(
    tc, x_words, x_scales, w1, w2, w3, offs, la, lb, out
):
    nc = tc.nc
    with ExitStack() as ctx:
        sb = ctx.enter_context(tc.tile_pool(name="sb", bufs=1))
        stage = ctx.enter_context(tc.tile_pool(name="stage", bufs=1))
        psum = ctx.enter_context(tc.psum_pool(name="psum", bufs=1))
        banks = [psum.tile([P, 512], F32, name=f"bank{b}") for b in range(8)]

        def product(acc, w_codes, w_scales, t, codes, scales):
            cols = slice(t * P, (t + 1) * P)
            nc.tensor.matmul_mx(
                out=acc,
                lhsT=w_codes[:, cols].bitcast(FP8X4),
                lhsT_scale=w_scales[:, cols],
                rhs=codes.bitcast(FP8X4),
                rhs_scale=scales,
                start=True,
                stop=True,
            )

        def quantize_weight(codes, scales, rounded, t0, t1):
            cols = slice(t0 * P, t1 * P)
            nc.vector.quantize_mx(
                out=codes[:, cols].bitcast(FP8X4),
                scales=scales[:, cols],
                in_=rounded[:, PACK * t0 * P : PACK * t1 * P],
            )

        def deal_to(rounded):
            return rounded[:].rearrange("p (t m j) -> p m j t", t=PACK, j=PACK)

        def deal_from(raw):
            return raw[:].rearrange("p j (m t) -> p m j t", t=PACK)

        offs_sb = sb.tile([P, S // 16], U16, name="offs_sb")
        la_sb = sb.tile([P, V // 16], U16, name="la_sb")
        lb_sb = sb.tile([P, V // 16], U16, name="lb_sb")
        xs_all = sb.tile([P, T], U8, name="xs_all", align_bytes=64)
        xw_all = sb.tile([P, T], I32, name="xw_all", align_bytes=64)
        w1_raw = [sb.tile([P, PACK, HALF], F32, name=f"w1_raw{u}") for u in range(2)]
        w2_raw = stage.tile([P, PACK, H], F32, name="w2_raw", offset=0, align_bytes=64)
        w3_raw = sb.tile([P, PACK, N], F32, name="w3_raw")

        nc.vector.memset(xs_all[:].bitcast(I32), 0)
        nc.sync.dma_start(offs_sb[:], offs)
        nc.sync.dma_start(out=xw_all[:], in_=x_words[0].rearrange("p c r -> p (c r)").bitcast(I32))
        for q in (0, 2, 1, 3):
            nc.sync.dma_start(
                out=xs_all[32 * q : 32 * q + 4, :].bitcast(I32),
                in_=x_scales[0, 4 * q : 4 * q + 4, :].bitcast(I32),
            )
        for u, cols in enumerate(HALVES):
            nc.sync.dma_start(out=w1_raw[u][:], in_=w1.rearrange("(p j) c -> p j c", j=PACK)[:, :, cols])
        nc.sync.dma_start(la_sb[:], la)
        nc.sync.dma_start(lb_sb[:], lb)
        nc.sync.dma_start(out=w2_raw[:], in_=w2.rearrange("(p j) c -> p j c", j=PACK))
        nc.sync.dma_start(out=w3_raw[:], in_=w3.rearrange("(p j) c -> p j c", j=PACK))

        xw = sb.tile([P, S], U32, name="xw", tag="xw_then_w2", align_bytes=64)
        xs = sb.tile([P, S], U8, name="xs", align_bytes=64)
        nc.vector.tensor_copy(xw[:], xw_all[:].bitcast(U32).indirect(offs_sb[:]))
        nc.vector.tensor_copy(xs[:], xs_all[:].indirect(offs_sb[:]))

        w1_bf = sb.tile([P, PACK * H], BF16, name="w1_bf", align_bytes=64)
        w1_codes = sb.tile([P, H], U32, name="w1_codes", align_bytes=64)
        w1_scales = sb.tile([P, H], U8, name="w1_scales", align_bytes=64)
        cut = M_HALF + W1_VECTOR_SHARE
        nc.scalar.copy(deal_to(w1_bf)[:, :M_HALF], deal_from(w1_raw[0]))
        nc.vector.tensor_copy(deal_to(w1_bf)[:, M_HALF:cut], deal_from(w1_raw[1])[:, :W1_VECTOR_SHARE])
        nc.scalar.copy(deal_to(w1_bf)[:, cut:], deal_from(w1_raw[1])[:, W1_VECTOR_SHARE:])
        for t0, t1 in ((0, 1), (1, 2), (2, 4)):
            quantize_weight(w1_codes, w1_scales, w1_bf, t0, t1)

        y = [sb.tile([P, S], F32, name=f"y{t}") for t in range(PACK)]
        for t in range(PACK):
            for u, cols in enumerate(HALVES):
                bank = banks[2 * t + u]
                product(bank[:, :HALF], w1_codes, w1_scales, t, xw[:, cols], xs[:, cols])
                copy = nc.vector.tensor_copy if (t, u) == (0, 1) else nc.scalar.copy
                copy(y[t][:, cols], bank[:, :HALF])

        w2_bf = sb.tile([P, PACK * H], BF16, name="w2_bf", tag="xw_then_w2", align_bytes=64)
        w2_codes = sb.tile([P, H], U32, name="w2_codes", align_bytes=64)
        w2_scales = sb.tile([P, H], U8, name="w2_scales", align_bytes=64)
        for m0 in range(0, P, P // W2_PIECES):
            ms = slice(m0, m0 + P // W2_PIECES)
            nc.scalar.copy(deal_to(w2_bf)[:, ms], deal_from(w2_raw)[:, ms])

        a = sb.tile([P, PACK, V], F32, name="a")
        pair_sum = sb.tile([P, PACK, V], F32, name="pair_sum")
        for t0 in (0, 2):
            for t in (t0, t0 + 1):
                nc.vector.tensor_copy(a[:, t, :], y[t][:].indirect(la_sb[:]))
            for t in (t0, t0 + 1):
                nc.vector.tensor_tensor(pair_sum[:, t, :], y[t][:].indirect(lb_sb[:]), a[:, t, :], ALU.add)

        quantize_weight(w2_codes, w2_scales, w2_bf, 3, 4)
        z_bf = stage.tile([P, V, PACK], BF16, name="z_bf", offset=0, align_bytes=64)
        sum_by_column = pair_sum[:].rearrange("p t v -> p v t")
        nc.scalar.activation(z_bf[:, :, 0:2], sum_by_column[:, :, 0:2], ACT.Copy, scale=0.75)
        nc.vector.tensor_scalar(z_bf[:, :, 2:4], sum_by_column[:, :, 2:4], 0.75, None, ALU.mult)
        quantize_weight(w2_codes, w2_scales, w2_bf, 0, 1)
        z_codes = sb.tile([P, V], U32, name="z_codes", tag="z_then_w3", align_bytes=64)
        z_scales = sb.tile([P, V], U8, name="z_scales", align_bytes=64)
        nc.vector.quantize_mx(
            out=z_codes[:].bitcast(FP8X4), scales=z_scales[:], in_=z_bf[:].rearrange("p v t -> p (v t)")
        )
        quantize_weight(w2_codes, w2_scales, w2_bf, 1, 3)

        twice_a = stage.tile([P, PACK, V], F32, name="twice_a", offset=PACK * V * 4, align_bytes=64)
        for t0 in (2, 0):
            nc.scalar.activation(twice_a[:, t0 : t0 + 2, :], a[:, t0 : t0 + 2, :], ACT.Copy, scale=2.0)
        df = stage.tile([P, PACK, V], F32, name="df", offset=0, align_bytes=64)
        neg_df_early = sb.tile([P, 2, V], F32, name="neg_df_early")
        neg_df = {3: neg_df_early[:, 0, :], 0: neg_df_early[:, 1, :]}
        h = sb.tile([P, PACK, V], F32, name="h")
        for t in SCATTER_ORDER:
            nc.vector.tensor_tensor(df[:, t, :], twice_a[:, t, :], pair_sum[:, t, :], ALU.subtract)
        for t in SCATTER_ORDER:
            product(banks[t][:, :V], w2_codes, w2_scales, t, z_codes[:], z_scales[:])
            nc.scalar.activation(h[:, t, :], banks[t][:, :V], ACT.Relu)
        for t in SCATTER_ORDER[:2]:
            nc.scalar.activation(neg_df[t], df[:, t, :], ACT.Copy, scale=-1.0)

        z2 = [sb.tile([P, 2 * S if t == 2 else S], F32, name=f"z2_{t}") for t in range(PACK - 1)]
        z2.append(sb.tile([P, S], F32, name="z2_3", tag="z2_3_then_neg_df_then_w3", align_bytes=64))
        z2_bf = sb.tile([P, S, PACK], BF16, name="z2_bf", align_bytes=64)

        def scatter_a(t):
            nc.vector.tensor_tensor(z2[t][:].indirect(la_sb[:]), h[:, t, :], df[:, t, :], ALU.add)

        def scatter_b(t):
            nc.vector.tensor_tensor(z2[t][:].indirect(lb_sb[:]), h[:, t, :], neg_df[t], ALU.add)

        def weave(t):
            for cols in HALVES:
                nc.scalar.copy(z2_bf[:, cols, t], z2[t][:, cols])

        scatter_a(3)
        scatter_a(0)
        scatter_b(3)
        nc.scalar.copy(z2[2][:, S:], z2[3][:])
        neg_df_late = sb.tile([P, 2, V], F32, name="neg_df_late", tag="z2_3_then_neg_df_then_w3", align_bytes=64)
        nc.scalar.activation(neg_df_late[:], df[:, 1:3, :], ACT.Copy, scale=-1.0)
        neg_df[1], neg_df[2] = neg_df_late[:, 0, :], neg_df_late[:, 1, :]
        w3_bf = sb.tile([P, PACK * N], BF16, name="w3_bf", tag="z_then_w3", align_bytes=64)
        for c0 in range(0, P, P // W3_PIECES):
            cs = slice(c0, c0 + P // W3_PIECES)
            nc.scalar.copy(
                w3_bf[:].rearrange("p (c i j) -> p c j i", i=4, j=PACK)[:, cs],
                w3_raw[:].rearrange("p j (c i) -> p c j i", i=4)[:, cs],
            )
        scatter_a(1)
        scatter_b(0)
        weave(0)
        scatter_a(2)
        scatter_b(1)
        weave(1)
        scatter_b(2)

        w3_codes = sb.tile([P, N], U32, name="w3_codes", tag="z2_3_then_neg_df_then_w3", align_bytes=64)
        w3_scales = sb.tile([P, N], U8, name="w3_scales", align_bytes=64)
        quantize_weight(w3_codes, w3_scales, w3_bf, 0, 1)
        tiles_2_3 = z2[2][:].rearrange("p (u c) -> p c u", u=2)
        nc.vector.tensor_copy(z2_bf[:, :HALF, 2:4], tiles_2_3[:, :HALF, :])
        nc.scalar.copy(z2_bf[:, HALF:, 2:4], tiles_2_3[:, HALF:, :])

        z2_codes = sb.tile([P, S], U32, name="z2_codes", align_bytes=64)
        z2_scales = sb.tile([P, S], U8, name="z2_scales", align_bytes=64)
        for cols, (t0, t1) in zip(HALVES, ((1, 2), (2, 4))):
            quantize_weight(w3_codes, w3_scales, w3_bf, t0, t1)
            nc.vector.quantize_mx(
                out=z2_codes[:, cols].bitcast(FP8X4),
                scales=z2_scales[:, cols],
                in_=z2_bf[:, cols, :].rearrange("p c t -> p (c t)"),
            )

        for u, cols in enumerate(HALVES):
            for t in range(PACK):
                result = sb.tile([P, HALF], F32, name=f"result{u}{t}")
                bank = banks[PACK * u + t]
                product(bank[:, :HALF], w3_codes, w3_scales, t, z2_codes[:, cols], z2_scales[:, cols])
                copy = nc.scalar.copy if t % 2 == 0 else nc.vector.tensor_copy
                copy(result[:], bank[:, :HALF])
                nc.sync.dma_start(out=out[t * P : (t + 1) * P, cols], in_=result[:])
